import numpy as np
import ml_dtypes


def mxq(x, axis, fmt="e4m3"):
    dtype, down = {"e4m3": (ml_dtypes.float8_e4m3fn, 7), "e5m2": (ml_dtypes.float8_e5m2, 14)}[fmt]
    v = np.moveaxis(np.asarray(x, np.float32).astype(ml_dtypes.bfloat16).astype(np.float64), axis, -1)
    blocks = v.reshape(v.shape[:-1] + (-1, 32))
    amax = np.abs(blocks).max(-1, keepdims=True)
    byte = np.maximum(np.where(amax > 0, np.frexp(amax)[1] - 1 + 127, 0) - down, 1)
    scale = np.exp2(byte - 127.0)
    codes = (blocks / scale).astype(np.float32).astype(dtype).astype(np.float64)
    return np.moveaxis((codes * scale).reshape(v.shape), -1, axis)


WIDE = False


def mx_kscale(k):
    if not WIDE:
        return np.ones(k)
    levels = np.array([10, -10, 5, -5, 0])
    if k % 512:
        return np.exp2(np.random.permutation(np.resize(levels, k // 32))).repeat(32)
    a = np.empty((k // 512, 16))
    for p in range(k // 512):
        a[p, :8] = np.random.permutation(np.resize(levels, 8))
        for g in range(8):
            far = levels[np.abs(levels - a[p, g]) >= 10]
            a[p, g + 8] = far[np.random.randint(len(far))]
    return np.exp2(a.ravel()).repeat(32)


BF16 = ml_dtypes.bfloat16


def bf(x):
    return np.asarray(x, np.float32).astype(BF16)


def f64(x):
    return np.asarray(x).astype(np.float64)


T, C = 1024, 1024


def setup_inputs():
    s, u = mx_kscale(C), mx_kscale(T)
    x = np.random.standard_normal((T, C))
    spread = 0.33 * np.random.standard_normal((C, C)) / np.sqrt(C)
    adapt = 0.33 * np.random.standard_normal((T, T)) / np.sqrt(T)
    suppress = 0.5 * np.random.standard_normal((C, C)) / np.sqrt(C)
    afferent = 1 + 0.1 * np.random.standard_normal((T, C))
    efferent = np.random.uniform(0.3, 1.0, (T, C))
    return {"x": bf(x * u[:, None] * s),
            "spread": bf(spread / s[:, None] * s),
            "adapt": bf(adapt / u * u[:, None]),
            "suppress": bf(suppress / s[:, None]),
            "afferent": bf(afferent / u[:, None] / s),
            "efferent": bf(efferent / u[:, None])}


def reference(x, spread, adapt, suppress, afferent, efferent):
    x = f64(x)
    h1 = x + (mxq(x, 1, "e4m3") @ mxq(f64(spread), 0, "e4m3"))
    h2 = h1 - (mxq(f64(adapt), 1, "e4m3") @ mxq(h1, 0, "e4m3"))
    sup = mxq(h2, 1, "e4m3") @ mxq(f64(suppress), 0, "e4m3")
    return f64(afferent) * h2 - f64(efferent) * sup

@@ -1,0 +1,364 @@
+from contextlib import ExitStack
+
+import concourse.mybir as mybir
+from concourse.masks import make_identity
+
+F32 = mybir.dt.float32
+BF16 = mybir.dt.bfloat16
+U32 = mybir.dt.uint32
+U8 = mybir.dt.uint8
+FP8X4 = mybir.dt.float8_e4m3fn_x4
+ALU = mybir.AluOpType
+
+P = 128
+T = 1024
+C = 1024
+FLOPS = 3 * 2 * T * C * C
+
+
+def tile_cochlear_spread_adapt_suppress_t1_kernel(
+    tc, x, spread, adapt, suppress, afferent, efferent, out
+):
+    nc = tc.nc
+    x_v = x.rearrange("(g p t) c -> p g t c", p=P, t=4)
+    ad_v = adapt.rearrange("(g p t) c -> p g t c", p=P, t=4)
+    af_v = afferent.rearrange("(g p t) c -> p g t c", p=P, t=4)
+    ef_v = efferent.rearrange("(g p t) c -> p g t c", p=P, t=4)
+    out_v = out.rearrange("(g p t) c -> p g t c", p=P, t=4)
+    sp_v = spread.rearrange("(q p j) c -> p q j c", p=P, j=4)
+    su_v = suppress.rearrange("(q p j) c -> p q j c", p=P, j=4)
+
+    with ExitStack() as ctx:
+        keep = ctx.enter_context(tc.tile_pool(name="keep", bufs=1))
+        stage = ctx.enter_context(tc.tile_pool(name="stage", bufs=2))
+        psum = ctx.enter_context(tc.psum_pool(name="psum", bufs=4))
+
+        def keep_tile(shape, dtype, tag, align=64):
+            return keep.tile(shape, dtype, name=tag, tag=tag, align_bytes=align)
+
+        ident = keep_tile([P, P], F32, "ident")
+        make_identity(nc, ident[:])
+
+        def load_rows(view, c, tag):
+            t_sb = keep_tile([P, 2, C], BF16, tag)
+            h = 2 * (c % 2)
+            nc.sync.dma_start(out=t_sb[:], in_=view[:, c // 2, h : h + 2, :])
+            return t_sb
+
+        def load_w(view, q, h, tag):
+            t_sb = keep_tile([P, 4, 512], BF16, tag)
+            nc.sync.dma_start(out=t_sb[:], in_=view[:, q, :, 512 * h : 512 * h + 512])
+            return t_sb
+
+        x_sb = {}
+        sp_sb = {}
+        ad_sb = {}
+        su_sb = {}
+        af_sb = {}
+        ef_sb = {}
+        x_sb[0] = load_rows(x_v, 0, "a0")
+        sp_sb[0, 0] = load_w(sp_v, 0, 0, "b00")
+        sp_sb[1, 0] = load_w(sp_v, 1, 0, "b10")
+        for c in (1, 2, 3):
+            x_sb[c] = load_rows(x_v, c, "a%d" % c)
+        sp_sb[0, 1] = load_w(sp_v, 0, 1, "b01")
+        sp_sb[1, 1] = load_w(sp_v, 1, 1, "b11")
+        for c in range(4):
+            ad_sb[c] = load_rows(ad_v, c, "c%d" % c)
+
+        def acc_tile():
+            return psum.tile([P, 512], F32, name="acc", tag="acc", bufs=5)
+
+        grouped = {}
+
+        def turn(src, i, key, copy):
+            words = src[i // 2][:, i % 2, :].bitcast(F32)
+            bank = psum.tile([P, 2, 2, P], F32, name="tr", tag="tr", bufs=3)
+            for q in range(2):
+                for u in range(2):
+                    nc.tensor.transpose(
+                        bank[:, q, u, :], words[:, 256 * q + u : 256 * (q + 1) : 2], ident[:]
+                    )
+            if i % 2 == 0:
+                grouped[key, i // 2] = stage.tile(
+                    [P, 2, 1024], BF16, name="rows_g", tag="rows_g", bufs=3, align_bytes=64
+                )
+            g_sb = grouped[key, i // 2]
+            copy(
+                out=g_sb[:, i % 2, :].bitcast(F32).rearrange("p (q r u) -> p q r u", q=2, u=2),
+                in_=bank[:].rearrange("p q u r -> p q r u"),
+            )
+
+        def quant(src_ap, words, tag):
+            codes = keep_tile([P, words], U32, tag + "_c")
+            scales = keep_tile([P, words], U8, tag + "_s")
+            nc.vector.quantize_mx(out=codes[:].bitcast(FP8X4), scales=scales[:], in_=src_ap)
+            return codes, scales
+
+        def quant_pair(key, pr):
+            return quant(
+                grouped[key, pr][:].rearrange("p i e -> p (i e)"), 512, "%s%d" % (key, pr)
+            )
+
+        def mx(acc, lhs, lhs0, rhs, rhs0, start, stop):
+            nc.tensor.matmul_mx(
+                out=acc[:],
+                lhsT=lhs[0][:, lhs0 : lhs0 + P].bitcast(FP8X4),
+                lhsT_scale=lhs[1][:, lhs0 : lhs0 + P],
+                rhs=rhs[0][:, rhs0 : rhs0 + 512].bitcast(FP8X4),
+                rhs_scale=rhs[1][:, rhs0 : rhs0 + 512],
+                start=start,
+                stop=stop,
+            )
+
+        w_g = {}
+
+        def weave(raw, key, permuted, shares):
+            g_sb = stage.tile([P, 2048], BF16, name="w_g", tag="w_g", bufs=4, align_bytes=64)
+            w_g[key] = g_sb
+            t0 = 0
+            for engine, n in shares:
+                if permuted:
+                    o_v = g_sb[:].rearrange("p (t m j) -> p t m j", t=4, j=4)[:, t0 : t0 + n]
+                    i_v = raw[:].rearrange("p j (m t) -> p t m j", t=4)[:, t0 : t0 + n]
+                else:
+                    o_v = g_sb[:].rearrange("p (n j) -> p n j", j=4)[:, P * t0 : P * (t0 + n)]
+                    i_v = raw[:].rearrange("p j n -> p n j")[:, P * t0 : P * (t0 + n)]
+                t0 += n
+                if engine == "v":
+                    nc.vector.tensor_copy(out=o_v, in_=i_v)
+                elif engine == "s":
+                    nc.scalar.copy(out=o_v, in_=i_v)
+                else:
+                    nc.gpsimd.tensor_scalar(
+                        out=o_v, in0=i_v, scalar1=1.0, scalar2=0.0, op0=ALU.mult, op1=ALU.add
+                    )
+
+        xc = {}
+        spc = {}
+        adc = {}
+        h1c = {}
+        suc = {}
+        h1f = {}
+        for i in range(8):
+            for h in range(2):
+                h1f[i // 4, h] = None
+
+        acc1 = {}
+
+        def spread_mm(i, h):
+            acc1[i, h] = acc_tile()
+            for q in range(2):
+                mx(acc1[i, h], xc[i // 2], 256 * (i % 2) + P * q, spc[q, h], 0, q == 0, q == 1)
+
+        def spread_add(i, h):
+            if i % 4 == 0:
+                h1f[i // 4, h] = keep_tile([P, 4, 512], F32, "h1f%d%d" % (i // 4, h))
+            nc.vector.tensor_tensor(
+                out=h1f[i // 4, h][:, i % 4, :].rearrange("p (t m) -> p t m", t=4),
+                in0=acc1[i, h][:].rearrange("p (t m) -> p t m", t=4),
+                in1=x_sb[i // 2][:, i % 2, 512 * h : 512 * h + 512].rearrange(
+                    "p (m t) -> p t m", t=4
+                ),
+                op=ALU.add,
+            )
+
+        h1g = {}
+
+        def h1_weave(g, h):
+            t_sb = stage.tile([P, 512, 4], BF16, name="h1g", tag="h1g", bufs=2, align_bytes=64)
+            for b in range(2):
+                nc.scalar.copy(
+                    out=t_sb[:, 256 * b : 256 * b + 256, :],
+                    in_=h1f[g, h][:, :, 256 * b : 256 * b + 256].rearrange("p t n -> p n t"),
+                )
+            h1g[g, h] = t_sb
+
+        def h1_quant(g, h):
+            h1c[g, h] = quant(h1g[g, h][:].rearrange("p n t -> p (n t)"), 512, "h1%d%d" % (g, h))
+
+        COPY = nc.scalar.copy
+        GAIN_G = ()
+        ON_GPSIMD = {(i, h) for i in range(7) for h in range(2)} | {(7, 0)}
+        turn(x_sb, 0, "x", COPY)
+        turn(x_sb, 1, "x", COPY)
+        weave(sp_sb[0, 0], "sp00", True, [("v", 4)])
+        xc[0] = quant_pair("x", 0)
+        weave(sp_sb[1, 0], "sp10", True, [("v", 2), ("s", 2)])
+        turn(x_sb, 2, "x", COPY)
+        turn(x_sb, 3, "x", COPY)
+        spc[0, 0] = quant(w_g["sp00"][:], 512, "sp00")
+        spc[1, 0] = quant(w_g["sp10"][:], 512, "sp10")
+        spread_mm(0, 0)
+        spread_mm(1, 0)
+        xc[1] = quant_pair("x", 1)
+        spread_add(0, 0)
+        spread_mm(2, 0)
+        turn(x_sb, 4, "x", COPY)
+        turn(x_sb, 5, "x", COPY)
+        spread_add(1, 0)
+        spread_add(2, 0)
+        spread_mm(3, 0)
+        xc[2] = quant_pair("x", 2)
+        spread_mm(4, 0)
+        turn(x_sb, 6, "x", COPY)
+        turn(x_sb, 7, "x", COPY)
+        spread_mm(5, 0)
+        weave(sp_sb[0, 1], "sp01", True, [("s", 2), ("v", 2)])
+        weave(sp_sb[1, 1], "sp11", True, [("g", 1), ("g", 1), ("s", 2)])
+        spread_add(3, 0)
+        spread_add(4, 0)
+        xc[3] = quant_pair("x", 3)
+        spread_add(5, 0)
+        h1_weave(0, 0)
+        spread_mm(6, 0)
+        spread_mm(7, 0)
+        spread_add(6, 0)
+        spread_add(7, 0)
+        spc[0, 1] = quant(w_g["sp01"][:], 512, "sp01")
+        spc[1, 1] = quant(w_g["sp11"][:], 512, "sp11")
+        for q in range(2):
+            for h in range(2):
+                su_sb[q, h] = load_w(su_v, q, h, "b%d%d" % (q, h))
+        spread_mm(0, 1)
+        spread_mm(1, 1)
+        turn(ad_sb, 0, "ad", COPY)
+        turn(ad_sb, 1, "ad", COPY)
+        h1_weave(1, 0)
+        weave(su_sb[0, 0], "su00", False, [("g", 1)] * 4)
+        spread_add(0, 1)
+        spread_mm(2, 1)
+        spread_add(1, 1)
+        spread_mm(3, 1)
+        spread_add(2, 1)
+        h1_quant(0, 0)
+        turn(ad_sb, 2, "ad", COPY)
+        turn(ad_sb, 3, "ad", COPY)
+        spread_mm(4, 1)
+        spread_mm(5, 1)
+        spread_add(3, 1)
+        adc[0] = quant_pair("ad", 0)
+        h1_weave(0, 1)
+        weave(su_sb[1, 0], "su10", False, [("g", 1)] * 4)
+        spread_add(4, 1)
+        h1_quant(1, 0)
+        spread_add(5, 1)
+        turn(ad_sb, 4, "ad", COPY)
+        turn(ad_sb, 5, "ad", COPY)
+        adc[1] = quant_pair("ad", 1)
+        spread_mm(6, 1)
+        spread_mm(7, 1)
+        spread_add(6, 1)
+        spread_add(7, 1)
+        h1_weave(1, 1)
+        turn(ad_sb, 6, "ad", COPY)
+        turn(ad_sb, 7, "ad", COPY)
+        for c in range(4):
+            af_sb[c] = load_rows(af_v, c, "c%d" % c)
+        for c in range(4):
+            ef_sb[c] = load_rows(ef_v, c, "a%d" % c)
+        h2f = {}
+        t1 = {}
+        h2c = {}
+
+        def adapt_sub(i, h):
+            if i not in h2f:
+                h2f[i] = stage.tile([P, 2, 512], F32, name="h2f", tag="h2f", bufs=4)
+            acc = acc_tile()
+            for q in range(2):
+                mx(acc, adc[i // 2], 256 * (i % 2) + P * q, h1c[q, h], 0, q == 0, q == 1)
+            nc.vector.tensor_tensor(
+                out=h2f[i][:, h, :],
+                in0=h1f[i // 4, h][:, i % 4, :],
+                in1=acc[:],
+                op=ALU.subtract,
+            )
+
+        def gain(i):
+            t1[i] = stage.tile([P, 2, 512], F32, name="t1", tag="t1", bufs=4)
+            for h in range(2):
+                (nc.gpsimd if (i, h) in GAIN_G else nc.vector).tensor_tensor(
+                    out=t1[i][:, h, :].rearrange("p (m t) -> p m t", t=4),
+                    in0=h2f[i][:, h, :].rearrange("p (t m) -> p m t", t=4),
+                    in1=af_sb[i // 2][:, i % 2, 512 * h : 512 * h + 512].rearrange(
+                        "p (m t) -> p m t", t=4
+                    ),
+                    op=ALU.mult,
+                )
+
+        h2g = {}
+
+        def h2_turn(i):
+            h2g[i] = stage.tile([P, 2, P, 4], BF16, name="h2g", tag="h2g", bufs=3, align_bytes=64)
+            for h in range(2):
+                bank = psum.tile([P, 4, P], F32, name="tr", tag="tr", bufs=3)
+                for t in range(4):
+                    nc.tensor.transpose(
+                        bank[:, t, :], h2f[i][:, h, P * t : P * t + P], ident[:]
+                    )
+                nc.scalar.copy(out=h2g[i][:, h, :, :], in_=bank[:].rearrange("p t r -> p r t"))
+
+        def h2_quant(i):
+            h2c[i] = quant(h2g[i][:].rearrange("p h r t -> p (h r t)"), 256, "h2%d" % i)
+
+        o_sb = {}
+        acc3 = {}
+
+        def suppress_mm(i):
+            for h in range(2):
+                acc3[i, h] = acc_tile()
+                for q in range(2):
+                    mx(acc3[i, h], h2c[i], P * q, suc[q, h], 0, q == 0, q == 1)
+
+        def gate(i):
+            o_sb[i] = stage.tile([P, 2, 512], F32, name="o", tag="o", bufs=4)
+            for h in range(2):
+                nc.vector.tensor_tensor(
+                    out=o_sb[i][:, h, :],
+                    in0=acc3[i, h][:],
+                    in1=ef_sb[i // 2][:, i % 2, 512 * h : 512 * h + 512],
+                    op=ALU.mult,
+                )
+
+        def finish(i):
+            for h in range(2):
+                eng = nc.gpsimd if (i, h) in ON_GPSIMD else nc.vector
+                eng.tensor_tensor(
+                    out=o_sb[i][:, h, :], in0=t1[i][:, h, :], in1=o_sb[i][:, h, :], op=ALU.subtract
+                )
+            nc.sync.dma_start(
+                out=out_v[:, i // 4, i % 4, :], in_=o_sb[i][:].rearrange("p h n -> p (h n)")
+            )
+
+
+        adapt_sub(0, 0)
+        adapt_sub(1, 0)
+        h1_quant(0, 1)
+        adc[2] = quant_pair("ad", 2)
+        h1_quant(1, 1)
+        adapt_sub(0, 1)
+        h2_turn(0)
+        adapt_sub(1, 1)
+        suc[0, 0] = quant(w_g["su00"][:], 512, "su00")
+        weave(su_sb[0, 1], "su01", False, [("s", 2), ("v", 2)])
+        weave(su_sb[1, 1], "su11", False, [("s", 2), ("v", 2)])
+        h2_quant(0)
+        suc[1, 0] = quant(w_g["su10"][:], 512, "su10")
+        suc[0, 1] = quant(w_g["su01"][:], 512, "su01")
+        suc[1, 1] = quant(w_g["su11"][:], 512, "su11")
+        adc[3] = quant_pair("ad", 3)
+        for step in range(2, 10):
+            if step < 8:
+                adapt_sub(step, 0)
+                adapt_sub(step, 1)
+            suppress_mm(step - 2)
+            if step <= 8:
+                h2_turn(step - 1)
+            gate(step - 2)
+            if step <= 8:
+                h2_quant(step - 1)
+            if step < 9:
+                gain(step - 2)
+            if step == 8:
+                gain(7)
+            finish(step - 2)

@@ -11,354 +11,579 @@ FP8X4 = mybir.dt.float8_e4m3fn_x4
 ALU = mybir.AluOpType
 
 P = 128
-T = 1024
 C = 1024
-FLOPS = 3 * 2 * T * C * C
+FLOPS = 3 * 2 * C * C * C
+
+ORDER = """
+ld x 0
+lw sp 0 0
+ld x 1
+lw sp 1 0
+ld x 2
+ld x 3
+lw sp 0 1
+lw sp 1 1
+ld ad 0
+turn x 0
+ld ad 1
+weave sp 0 0 3 s
+weave sp 0 0 1 g
+evac x 0 1 v
+evac x 0 0 s
+weave sp 0 0 2 g
+ld ad 2
+turn x 1
+weave sp 0 0 0 s
+qr x 0
+weave sp 1 0 1 v
+ld ad 3
+weave sp 1 0 2 s
+weave sp 1 0 3 v
+evac x 1 0 s
+weave sp 1 0 0 v
+turn x 2
+evac x 1 1 s
+qw sp 0 0
+qr x 1
+turn x 3
+evac x 2 1 s
+qw sp 1 0
+evac x 2 0 s
+weave sp 0 1 3 v
+s1 0 0 3
+weave sp 0 1 0 s
+qr x 2
+s1 0 0 1
+weave sp 0 1 2 s
+weave sp 1 1 3 g
+a1 0 0 3
+s1 0 0 2
+weave sp 0 1 1 s
+a1 0 0 1
+s1 0 0 0
+evac x 3 1 s
+a1 0 0 2
+turn ad 0
+lu 0 0
+lu 0 1
+lu 0 2
+lu 0 3
+lu 0 4
+evac x 3 0 s
+a1 0 0 0
+lu 0 5
+weave sp 1 1 2 s
+qr x 3
+turn ad 1
+evac ad 0 0 s
+qh 0 0
+lu 0 6
+s1 1 0 1
+weave sp 1 1 0 s
+qw sp 0 1
+s1 1 0 3
+evac ad 1 0 s
+lu 0 7
+a1 1 0 1
+s1 1 0 0
+evac ad 0 1 s
+a1 1 0 3
+s1 1 0 2
+weave sp 1 1 1 s
+a1 1 0 0
+turn ad 2
+evac ad 1 1 s
+lu 1 0
+lu 1 1
+qr ad 0
+lu 1 2
+lu 1 3
+lu 1 4
+lu 1 5
+lu 1 6
+qw sp 1 1
+turn ad 3
+lu 1 7
+weave su 0 0 3 s
+weave su 0 0 1 v
+weave su 0 0 0 s
+weave su 0 1 3 g
+a1 1 0 2
+s1 0 1 1
+weave su 0 1 2 s
+s1 1 1 0
+weave su 0 1 1 g
+a1 0 1 1
+ld af 0
+evac ad 2 0 s
+s1 0 1 0
+ld af 1
+qh 1 0
+ld af 2
+weave su 0 1 0 s
+s1 1 1 3
+ld af 3
+ld ef 0
+a1 1 1 0
+s2 0 0
+weave su 0 0 2 s
+ld ef 1
+ld ef 2
+a1 1 1 3
+ld ef 3
+weave su 1 0 2 g
+weave su 1 1 1 s
+a1 0 1 0
+s1 0 1 2
+weave su 1 0 0 s
+weave su 1 1 2 g
+a2 0 0
+s1 1 1 1
+weave su 1 0 3 s
+weave su 1 1 3 g
+a1 0 1 2
+s1 0 1 3
+evac ad 2 1 s
+weave su 1 0 1 g
+a1 1 1 1
+s1 1 1 2
+evac ad 3 0 s
+s2 1 0
+a1 0 1 3
+weave su 1 1 0 g
+evac ad 3 1 s
+a1 1 1 2
+qw su 0 0
+qh 1 1
+qr ad 1
+qh 0 1
+s2 2 0
+qr ad 2
+s2 1 1
+qw su 1 0
+a2 2 0
+s2 0 1
+a2 1 0
+qw su 0 1
+s2 2 1
+a2 0 1
+t1 1 0 g
+a2 1 1
+ht 0
+qr ad 3
+ht 1
+a2 2 1
+t1 1 1 g
+he 0 0 s
+s2 3 0
+he 1 1 s
+he 1 0 v
+he 0 1 s
+qw su 1 1
+s2 3 1
+hq 1
+a2 3 0
+s3 1 1
+hq 0
+a2 3 1
+t1 3 0 g
+ht 2
+gt 1 1
+s3 0 1
+he 2 0 s
+t1 0 1 v
+ht 3
+he 2 1 s
+t1 0 0 v
+s3 0 0
+hq 2
+he 3 1 s
+gt 0 1
+fin 1 1 g
+s3 2 0
+he 3 0 s
+gt 0 0
+s3 1 0
+fin 0 1 g
+gt 2 0
+s3 2 1
+s2 4 0
+gt 1 0
+fin 0 0 v
+s2 4 1
+gt 2 1
+fin 1 0 g
+st 0 0
+st 0 1
+a2 4 0
+s2 5 1
+hq 3
+st 1 0
+st 1 1
+t1 2 0 v
+s3 3 1
+t1 4 0 v
+s2 5 0
+a2 4 1
+fin 2 0 g
+gt 3 1
+ht 4
+t1 4 1 g
+a2 5 0
+st 2 0
+s2 6 0
+a2 5 1
+he 4 0 s
+t1 3 1 v
+he 4 1 s
+s3 3 0
+t1 2 1 v
+s2 6 1
+hq 4
+gt 3 0
+fin 3 1 g
+s3 4 1
+a2 6 0
+ht 5
+fin 2 1 g
+a2 6 1
+gt 4 1
+s3 4 0
+he 5 0 s
+fin 3 0 g
+s2 7 1
+st 2 1
+he 5 1 s
+gt 4 0
+hq 5
+ht 6
+st 3 0
+st 3 1
+t1 5 0 v
+s3 5 1
+t1 5 1 v
+he 6 0 s
+s2 7 0
+a2 7 1
+fin 4 0 g
+he 6 1 s
+gt 5 1
+s3 5 0
+fin 4 1 g
+a2 7 0
+st 4 0
+gt 5 0
+ht 7
+hq 6
+st 4 1
+fin 5 1 v
+s3 6 0
+he 7 1 s
+t1 6 1 v
+s3 6 1
+he 7 0 s
+t1 6 0 v
+hq 7
+gt 6 1
+fin 5 0 g
+s3 7 1
+gt 6 0
+s3 7 0
+fin 6 1 g
+gt 7 1
+st 5 0
+st 5 1
+gt 7 0
+fin 6 0 v
+t1 7 0 v
+st 6 0
+st 6 1
+t1 7 1 v
+fin 7 0 v
+fin 7 1 v
+st 7 0
+st 7 1
+"""
 
 
 def tile_cochlear_spread_adapt_suppress_t1_kernel(
     tc, x, spread, adapt, suppress, afferent, efferent, out
 ):
     nc = tc.nc
-    x_v = x.rearrange("(g p t) c -> p g t c", p=P, t=4)
-    ad_v = adapt.rearrange("(g p t) c -> p g t c", p=P, t=4)
-    af_v = afferent.rearrange("(g p t) c -> p g t c", p=P, t=4)
-    ef_v = efferent.rearrange("(g p t) c -> p g t c", p=P, t=4)
-    out_v = out.rearrange("(g p t) c -> p g t c", p=P, t=4)
-    sp_v = spread.rearrange("(q p j) c -> p q j c", p=P, j=4)
-    su_v = suppress.rearrange("(q p j) c -> p q j c", p=P, j=4)
+    rows = {}
+    for key, ap in (("x", x), ("ad", adapt), ("af", afferent), ("ef", efferent), ("out", out)):
+        rows[key] = ap.rearrange("(g p t) c -> p g t c", p=P, t=4)
+    wts = {}
+    for key, ap in (("sp", spread), ("su", suppress)):
+        wts[key] = ap.rearrange("(q p j) c -> p q j c", p=P, j=4)
 
     with ExitStack() as ctx:
         keep = ctx.enter_context(tc.tile_pool(name="keep", bufs=1))
         stage = ctx.enter_context(tc.tile_pool(name="stage", bufs=2))
         psum = ctx.enter_context(tc.psum_pool(name="psum", bufs=4))
+        ctx.enter_context(tc.manual_schedule())
+        engines = {"v": nc.vector, "s": nc.scalar, "g": nc.gpsimd}
 
-        def keep_tile(shape, dtype, tag, align=64):
-            return keep.tile(shape, dtype, name=tag, tag=tag, align_bytes=align)
+        def keep_tile(shape, dtype, tag):
+            return keep.tile(shape, dtype, name=tag, tag=tag, align_bytes=64)
+
+        def stage_tile(shape, dtype, tag, bufs):
+            return stage.tile(shape, dtype, name=tag, tag=tag, bufs=bufs, align_bytes=64)
 
         ident = keep_tile([P, P], F32, "ident")
         make_identity(nc, ident[:])
+        raw = {}
+        bank = {}
+        woven = {}
+        codes = {}
+        h2f = {}
+        t1 = {}
+        o_sb = {}
 
-        def load_rows(view, c, tag):
-            t_sb = keep_tile([P, 2, C], BF16, tag)
-            h = 2 * (c % 2)
-            nc.sync.dma_start(out=t_sb[:], in_=view[:, c // 2, h : h + 2, :])
-            return t_sb
-
-        def load_w(view, q, h, tag):
-            t_sb = keep_tile([P, 4, 512], BF16, tag)
-            nc.sync.dma_start(out=t_sb[:], in_=view[:, q, :, 512 * h : 512 * h + 512])
-            return t_sb
-
-        x_sb = {}
-        sp_sb = {}
-        ad_sb = {}
-        su_sb = {}
-        af_sb = {}
-        ef_sb = {}
-        x_sb[0] = load_rows(x_v, 0, "a0")
-        sp_sb[0, 0] = load_w(sp_v, 0, 0, "b00")
-        sp_sb[1, 0] = load_w(sp_v, 1, 0, "b10")
-        for c in (1, 2, 3):
-            x_sb[c] = load_rows(x_v, c, "a%d" % c)
-        sp_sb[0, 1] = load_w(sp_v, 0, 1, "b01")
-        sp_sb[1, 1] = load_w(sp_v, 1, 1, "b11")
-        for c in range(4):
-            ad_sb[c] = load_rows(ad_v, c, "c%d" % c)
-
-        def acc_tile():
-            return psum.tile([P, 512], F32, name="acc", tag="acc", bufs=5)
-
-        grouped = {}
-
-        def turn(src, i, key, copy):
-            words = src[i // 2][:, i % 2, :].bitcast(F32)
-            bank = psum.tile([P, 2, 2, P], F32, name="tr", tag="tr", bufs=3)
-            for q in range(2):
-                for u in range(2):
-                    nc.tensor.transpose(
-                        bank[:, q, u, :], words[:, 256 * q + u : 256 * (q + 1) : 2], ident[:]
-                    )
-            if i % 2 == 0:
-                grouped[key, i // 2] = stage.tile(
-                    [P, 2, 1024], BF16, name="rows_g", tag="rows_g", bufs=3, align_bytes=64
+        def negate(engine, out, in_):
+            if engine == "s":
+                nc.scalar.mul(out, in_, -1.0)
+            elif engine == "v":
+                nc.vector.tensor_scalar_mul(out, in_, -1.0)
+            else:
+                nc.gpsimd.tensor_scalar(
+                    out=out, in0=in_, scalar1=-1.0, scalar2=0.0, op0=ALU.mult, op1=ALU.add
                 )
-            g_sb = grouped[key, i // 2]
+
+        def copy(engine, out, in_):
+            if engine == "s":
+                nc.scalar.copy(out=out, in_=in_)
+            elif engine == "v":
+                nc.vector.tensor_copy(out=out, in_=in_)
+            else:
+                nc.gpsimd.tensor_scalar(
+                    out=out, in0=in_, scalar1=1.0, scalar2=0.0, op0=ALU.mult, op1=ALU.add
+                )
+
+        SLOT = {"x": "a", "ad": "c", "af": "c", "ef": "e"}
+
+        def load_rows(key, c):
+            c = int(c)
+            g = c // 2
+            h = 2 * (c % 2)
+            if h == 0:
+                raw[key, g] = keep_tile([P, 4, C], BF16, "%s%d" % (SLOT[key], g))
+            nc.sync.dma_start(out=raw[key, g][:, h : h + 2, :], in_=rows[key][:, g, h : h + 2, :])
+
+        def load_su(q, i):
+            q, i = int(q), int(i)
+            if i == 0:
+                raw["su", q] = keep_tile([P, 4, C], BF16, "b%d" % q)
+            nc.sync.dma_start(
+                out=raw["su", q][i:P:8, :, :],
+                in_=suppress[512 * q : 512 * q + 512, :].rearrange(
+                    "(b j i) c -> i b j c", j=4, i=8
+                )[i],
+            )
+
+        def load_wt(key, q, h):
+            q, h = int(q), int(h)
+            if h == 0:
+                raw[key, q] = keep_tile([P, 4, C], BF16, "b%d" % q)
+            nc.sync.dma_start(
+                out=raw[key, q][:, :, 512 * h : 512 * h + 512],
+                in_=wts[key][:, q, :, 512 * h : 512 * h + 512],
+            )
+
+        def turn(key, pr):
+            b = psum.tile([P, 2, 2, 2, P], F32, name="tr", tag="tr", bufs=2)
+            bank[key, pr] = b
+            for k in range(2):
+                i = 2 * int(pr) + k
+                words = raw[key, i // 4][:, i % 4, :].bitcast(F32)
+                for q in range(2):
+                    for u in range(2):
+                        nc.tensor.transpose(
+                            b[:, k, q, u, :], words[:, 256 * q + u : 256 * (q + 1) : 2], ident[:]
+                        )
+
+        def evac(key, pr, k, engine):
+            k = int(k)
+            if (key, pr) not in woven:
+                woven[key, pr] = stage_tile([P, 2, 1024], BF16, "rows_g", 3)
             copy(
-                out=g_sb[:, i % 2, :].bitcast(F32).rearrange("p (q r u) -> p q r u", q=2, u=2),
-                in_=bank[:].rearrange("p q u r -> p q r u"),
+                engine,
+                woven[key, pr][:, k, :].bitcast(F32).rearrange("p (q r u) -> p q r u", q=2, u=2),
+                bank[key, pr][:, k].rearrange("p q u r -> p q r u"),
             )
 
-        def quant(src_ap, words, tag):
-            codes = keep_tile([P, words], U32, tag + "_c")
-            scales = keep_tile([P, words], U8, tag + "_s")
-            nc.vector.quantize_mx(out=codes[:].bitcast(FP8X4), scales=scales[:], in_=src_ap)
-            return codes, scales
+        def quantize(name, src_ap, words, pool_tile):
+            c_t = pool_tile([P, words], U32, "c" + name)
+            s_t = pool_tile([P, words], U8, "s" + name)
+            nc.vector.quantize_mx(out=c_t[:].bitcast(FP8X4), scales=s_t[:], in_=src_ap)
+            codes[name] = (c_t, s_t)
 
-        def quant_pair(key, pr):
-            return quant(
-                grouped[key, pr][:].rearrange("p i e -> p (i e)"), 512, "%s%d" % (key, pr)
+        def quant_rows(key, pr):
+            quantize(
+                key + pr, woven[key, pr][:].rearrange("p i e -> p (i e)"), 512, keep_tile
             )
 
-        def mx(acc, lhs, lhs0, rhs, rhs0, start, stop):
+        def weave(key, q, h, t, engine):
+            q, h, t = int(q), int(h), int(t)
+            if (key, q, h) not in woven:
+                woven[key, q, h] = stage_tile([P, 2048], BF16, "w_g", 4)
+            src = raw[key, q][:, :, 512 * h : 512 * h + 512]
+            if key == "sp":
+                o_v = woven[key, q, h][:].rearrange("p (t b i j) -> p t b i j", t=4, b=16, j=4)[:, t]
+                i_v = src.rearrange("p j (b t i) -> p t b i j", b=16, t=4)[:, t]
+            else:
+                o_v = woven[key, q, h][:].rearrange("p (n j) -> p n j", j=4)
+                o_v = o_v[:, P * t : P * (t + 1)]
+                i_v = src.rearrange("p j n -> p n j")[:, P * t : P * (t + 1)]
+            (negate if key == "sp" else copy)(engine, o_v, i_v)
+
+        def quant_wt(key, q, h):
+            quantize(key + q + h, woven[key, int(q), int(h)][:], 512, keep_tile)
+
+        def mx(acc_ap, lhs, l0, rhs, r0, n, start, stop):
             nc.tensor.matmul_mx(
-                out=acc[:],
-                lhsT=lhs[0][:, lhs0 : lhs0 + P].bitcast(FP8X4),
-                lhsT_scale=lhs[1][:, lhs0 : lhs0 + P],
-                rhs=rhs[0][:, rhs0 : rhs0 + 512].bitcast(FP8X4),
-                rhs_scale=rhs[1][:, rhs0 : rhs0 + 512],
+                out=acc_ap,
+                lhsT=codes[lhs][0][:, l0 : l0 + P].bitcast(FP8X4),
+                lhsT_scale=codes[lhs][1][:, l0 : l0 + P],
+                rhs=codes[rhs][0][:, r0 : r0 + n].bitcast(FP8X4),
+                rhs_scale=codes[rhs][1][:, r0 : r0 + n],
                 start=start,
                 stop=stop,
             )
 
-        w_g = {}
+        def acc_tile(key):
+            bank[key] = psum.tile([P, 512], F32, name="acc", tag="acc", bufs=4)
+            return bank[key]
 
-        def weave(raw, key, permuted, shares):
-            g_sb = stage.tile([P, 2048], BF16, name="w_g", tag="w_g", bufs=4, align_bytes=64)
-            w_g[key] = g_sb
-            t0 = 0
-            for engine, n in shares:
-                if permuted:
-                    o_v = g_sb[:].rearrange("p (t m j) -> p t m j", t=4, j=4)[:, t0 : t0 + n]
-                    i_v = raw[:].rearrange("p j (m t) -> p t m j", t=4)[:, t0 : t0 + n]
-                else:
-                    o_v = g_sb[:].rearrange("p (n j) -> p n j", j=4)[:, P * t0 : P * (t0 + n)]
-                    i_v = raw[:].rearrange("p j n -> p n j")[:, P * t0 : P * (t0 + n)]
-                t0 += n
-                if engine == "v":
-                    nc.vector.tensor_copy(out=o_v, in_=i_v)
-                elif engine == "s":
-                    nc.scalar.copy(out=o_v, in_=i_v)
-                else:
-                    nc.gpsimd.tensor_scalar(
-                        out=o_v, in0=i_v, scalar1=1.0, scalar2=0.0, op0=ALU.mult, op1=ALU.add
-                    )
-
-        xc = {}
-        spc = {}
-        adc = {}
-        h1c = {}
-        suc = {}
-        h1f = {}
-        for i in range(8):
-            for h in range(2):
-                h1f[i // 4, h] = None
-
-        acc1 = {}
-
-        def spread_mm(i, h):
-            acc1[i, h] = acc_tile()
-            for q in range(2):
-                mx(acc1[i, h], xc[i // 2], 256 * (i % 2) + P * q, spc[q, h], 0, q == 0, q == 1)
-
-        def spread_add(i, h):
-            if i % 4 == 0:
-                h1f[i // 4, h] = keep_tile([P, 4, 512], F32, "h1f%d%d" % (i // 4, h))
-            nc.vector.tensor_tensor(
-                out=h1f[i // 4, h][:, i % 4, :].rearrange("p (t m) -> p t m", t=4),
-                in0=acc1[i, h][:].rearrange("p (t m) -> p t m", t=4),
-                in1=x_sb[i // 2][:, i % 2, 512 * h : 512 * h + 512].rearrange(
-                    "p (m t) -> p t m", t=4
-                ),
-                op=ALU.add,
+        def x_perm(i, h):
+            return raw["x", i // 4][:, i % 4, 512 * h : 512 * h + 512].rearrange(
+                "p (b j i) -> p j b i", b=16, j=4
             )
 
-        h1g = {}
+        def spread_mm(g, h, j):
+            g = int(g)
+            acc = psum.tile([P, 4, P], F32, name="acc", tag="acc", bufs=4)
+            bank["s1", g, h, j] = acc
+            for t in range(4):
+                i = 4 * g + t
+                for q in range(2):
+                    mx(
+                        acc[:, t, :], "x%d" % (i // 2), 256 * (i % 2) + P * q,
+                        "sp%d%s" % (q, h), P * int(j), P, q == 0, q == 1,
+                    )
 
-        def h1_weave(g, h):
-            t_sb = stage.tile([P, 512, 4], BF16, name="h1g", tag="h1g", bufs=2, align_bytes=64)
-            for b in range(2):
-                nc.scalar.copy(
-                    out=t_sb[:, 256 * b : 256 * b + 256, :],
-                    in_=h1f[g, h][:, :, 256 * b : 256 * b + 256].rearrange("p t n -> p n t"),
-                )
-            h1g[g, h] = t_sb
-
-        def h1_quant(g, h):
-            h1c[g, h] = quant(h1g[g, h][:].rearrange("p n t -> p (n t)"), 512, "h1%d%d" % (g, h))
-
-        COPY = nc.scalar.copy
-        GAIN_G = ()
-        ON_GPSIMD = {(i, h) for i in range(7) for h in range(2)} | {(7, 0)}
-        turn(x_sb, 0, "x", COPY)
-        turn(x_sb, 1, "x", COPY)
-        weave(sp_sb[0, 0], "sp00", True, [("v", 4)])
-        xc[0] = quant_pair("x", 0)
-        weave(sp_sb[1, 0], "sp10", True, [("v", 2), ("s", 2)])
-        turn(x_sb, 2, "x", COPY)
-        turn(x_sb, 3, "x", COPY)
-        spc[0, 0] = quant(w_g["sp00"][:], 512, "sp00")
-        spc[1, 0] = quant(w_g["sp10"][:], 512, "sp10")
-        spread_mm(0, 0)
-        spread_mm(1, 0)
-        xc[1] = quant_pair("x", 1)
-        spread_add(0, 0)
-        spread_mm(2, 0)
-        turn(x_sb, 4, "x", COPY)
-        turn(x_sb, 5, "x", COPY)
-        spread_add(1, 0)
-        spread_add(2, 0)
-        spread_mm(3, 0)
-        xc[2] = quant_pair("x", 2)
-        spread_mm(4, 0)
-        turn(x_sb, 6, "x", COPY)
-        turn(x_sb, 7, "x", COPY)
-        spread_mm(5, 0)
-        weave(sp_sb[0, 1], "sp01", True, [("s", 2), ("v", 2)])
-        weave(sp_sb[1, 1], "sp11", True, [("g", 1), ("g", 1), ("s", 2)])
-        spread_add(3, 0)
-        spread_add(4, 0)
-        xc[3] = quant_pair("x", 3)
-        spread_add(5, 0)
-        h1_weave(0, 0)
-        spread_mm(6, 0)
-        spread_mm(7, 0)
-        spread_add(6, 0)
-        spread_add(7, 0)
-        spc[0, 1] = quant(w_g["sp01"][:], 512, "sp01")
-        spc[1, 1] = quant(w_g["sp11"][:], 512, "sp11")
-        for q in range(2):
-            for h in range(2):
-                su_sb[q, h] = load_w(su_v, q, h, "b%d%d" % (q, h))
-        spread_mm(0, 1)
-        spread_mm(1, 1)
-        turn(ad_sb, 0, "ad", COPY)
-        turn(ad_sb, 1, "ad", COPY)
-        h1_weave(1, 0)
-        weave(su_sb[0, 0], "su00", False, [("g", 1)] * 4)
-        spread_add(0, 1)
-        spread_mm(2, 1)
-        spread_add(1, 1)
-        spread_mm(3, 1)
-        spread_add(2, 1)
-        h1_quant(0, 0)
-        turn(ad_sb, 2, "ad", COPY)
-        turn(ad_sb, 3, "ad", COPY)
-        spread_mm(4, 1)
-        spread_mm(5, 1)
-        spread_add(3, 1)
-        adc[0] = quant_pair("ad", 0)
-        h1_weave(0, 1)
-        weave(su_sb[1, 0], "su10", False, [("g", 1)] * 4)
-        spread_add(4, 1)
-        h1_quant(1, 0)
-        spread_add(5, 1)
-        turn(ad_sb, 4, "ad", COPY)
-        turn(ad_sb, 5, "ad", COPY)
-        adc[1] = quant_pair("ad", 1)
-        spread_mm(6, 1)
-        spread_mm(7, 1)
-        spread_add(6, 1)
-        spread_add(7, 1)
-        h1_weave(1, 1)
-        turn(ad_sb, 6, "ad", COPY)
-        turn(ad_sb, 7, "ad", COPY)
-        for c in range(4):
-            af_sb[c] = load_rows(af_v, c, "c%d" % c)
-        for c in range(4):
-            ef_sb[c] = load_rows(ef_v, c, "a%d" % c)
-        h2f = {}
-        t1 = {}
-        h2c = {}
-
-        def adapt_sub(i, h):
-            if i not in h2f:
-                h2f[i] = stage.tile([P, 2, 512], F32, name="h2f", tag="h2f", bufs=4)
-            acc = acc_tile()
-            for q in range(2):
-                mx(acc, adc[i // 2], 256 * (i % 2) + P * q, h1c[q, h], 0, q == 0, q == 1)
+        def spread_out(g, h, j):
+            g, hh, jj = int(g), int(h), int(j)
+            if ("h1", g, h) not in woven:
+                woven["h1", g, h] = stage_tile([P, 512, 4], BF16, "h1g", 3)
             nc.vector.tensor_tensor(
-                out=h2f[i][:, h, :],
-                in0=h1f[i // 4, h][:, i % 4, :],
-                in1=acc[:],
+                out=woven["h1", g, h][:, P * jj : P * jj + P, :].rearrange(
+                    "p (b i) t -> p b i t", i=8
+                ),
+                in0=raw["x", g][:, :, 512 * hh : 512 * hh + 512].rearrange(
+                    "p t (b j i) -> p j b i t", b=16, j=4
+                )[:, jj],
+                in1=bank["s1", g, h, j][:].rearrange("p t (b i) -> p b i t", i=8),
                 op=ALU.subtract,
             )
 
-        def gain(i):
-            t1[i] = stage.tile([P, 2, 512], F32, name="t1", tag="t1", bufs=4)
-            for h in range(2):
-                (nc.gpsimd if (i, h) in GAIN_G else nc.vector).tensor_tensor(
-                    out=t1[i][:, h, :].rearrange("p (m t) -> p m t", t=4),
-                    in0=h2f[i][:, h, :].rearrange("p (t m) -> p m t", t=4),
-                    in1=af_sb[i // 2][:, i % 2, 512 * h : 512 * h + 512].rearrange(
-                        "p (m t) -> p m t", t=4
-                    ),
-                    op=ALU.mult,
-                )
-
-        h2g = {}
-
-        def h2_turn(i):
-            h2g[i] = stage.tile([P, 2, P, 4], BF16, name="h2g", tag="h2g", bufs=3, align_bytes=64)
-            for h in range(2):
-                bank = psum.tile([P, 4, P], F32, name="tr", tag="tr", bufs=3)
-                for t in range(4):
-                    nc.tensor.transpose(
-                        bank[:, t, :], h2f[i][:, h, P * t : P * t + P], ident[:]
-                    )
-                nc.scalar.copy(out=h2g[i][:, h, :, :], in_=bank[:].rearrange("p t r -> p r t"))
-
-        def h2_quant(i):
-            h2c[i] = quant(h2g[i][:].rearrange("p h r t -> p (h r t)"), 256, "h2%d" % i)
-
-        o_sb = {}
-        acc3 = {}
-
-        def suppress_mm(i):
-            for h in range(2):
-                acc3[i, h] = acc_tile()
-                for q in range(2):
-                    mx(acc3[i, h], h2c[i], P * q, suc[q, h], 0, q == 0, q == 1)
-
-        def gate(i):
-            o_sb[i] = stage.tile([P, 2, 512], F32, name="o", tag="o", bufs=4)
-            for h in range(2):
-                nc.vector.tensor_tensor(
-                    out=o_sb[i][:, h, :],
-                    in0=acc3[i, h][:],
-                    in1=ef_sb[i // 2][:, i % 2, 512 * h : 512 * h + 512],
-                    op=ALU.mult,
-                )
-
-        def finish(i):
-            for h in range(2):
-                eng = nc.gpsimd if (i, h) in ON_GPSIMD else nc.vector
-                eng.tensor_tensor(
-                    out=o_sb[i][:, h, :], in0=t1[i][:, h, :], in1=o_sb[i][:, h, :], op=ALU.subtract
-                )
-            nc.sync.dma_start(
-                out=out_v[:, i // 4, i % 4, :], in_=o_sb[i][:].rearrange("p h n -> p (h n)")
+        def h1_quant(g, h):
+            quantize(
+                "h" + g + h, woven["h1", int(g), h][:].rearrange("p n t -> p (n t)"), 512,
+                keep_tile,
             )
 
+        def adapt_mm(i, h):
+            i = int(i)
+            acc = acc_tile(("s2", i, h))
+            l0 = 256 * (i % 2)
+            for q in range(2):
+                mx(acc[:], "x%d" % (i // 2), l0 + P * q, "sp%d%s" % (q, h), 0, 512, q == 0, False)
+            for q in range(2):
+                mx(acc[:], "ad%d" % (i // 2), l0 + P * q, "h%d%s" % (q, h), 0, 512, False, q == 1)
 
-        adapt_sub(0, 0)
-        adapt_sub(1, 0)
-        h1_quant(0, 1)
-        adc[2] = quant_pair("ad", 2)
-        h1_quant(1, 1)
-        adapt_sub(0, 1)
-        h2_turn(0)
-        adapt_sub(1, 1)
-        suc[0, 0] = quant(w_g["su00"][:], 512, "su00")
-        weave(su_sb[0, 1], "su01", False, [("s", 2), ("v", 2)])
-        weave(su_sb[1, 1], "su11", False, [("s", 2), ("v", 2)])
-        h2_quant(0)
-        suc[1, 0] = quant(w_g["su10"][:], 512, "su10")
-        suc[0, 1] = quant(w_g["su01"][:], 512, "su01")
-        suc[1, 1] = quant(w_g["su11"][:], 512, "su11")
-        adc[3] = quant_pair("ad", 3)
-        for step in range(2, 10):
-            if step < 8:
-                adapt_sub(step, 0)
-                adapt_sub(step, 1)
-            suppress_mm(step - 2)
-            if step <= 8:
-                h2_turn(step - 1)
-            gate(step - 2)
-            if step <= 8:
-                h2_quant(step - 1)
-            if step < 9:
-                gain(step - 2)
-            if step == 8:
-                gain(7)
-            finish(step - 2)
+        def adapt_out(i, h):
+            i, hh = int(i), int(h)
+            if i not in h2f:
+                h2f[i] = stage_tile([P, 2, 512], F32, "h2f", 5)
+            nc.vector.tensor_tensor(
+                out=h2f[i][:, hh, :].rearrange("p (j b i) -> p j b i", j=4, b=16),
+                in0=x_perm(i, hh),
+                in1=bank["s2", i, h][:].rearrange("p (j b i) -> p j b i", j=4, b=16),
+                op=ALU.subtract,
+            )
+
+        def h2_turn(i):
+            b = psum.tile([P, 2, 4, P], F32, name="tr", tag="tr", bufs=2)
+            bank["h2", i] = b
+            for h in range(2):
+                for t in range(4):
+                    nc.tensor.transpose(
+                        b[:, h, t, :], h2f[int(i)][:, h, P * t : P * t + P], ident[:]
+                    )
+
+        def h2_evac(i, h, engine):
+            h = int(h)
+            if ("h2", i) not in woven:
+                woven["h2", i] = stage_tile([P, 2, P, 4], BF16, "h2g", 3)
+            copy(engine, woven["h2", i][:, h], bank["h2", i][:, h].rearrange("p t r -> p r t"))
+
+        def h2_quant(i):
+            quantize(
+                "k" + i, woven["h2", i][:].rearrange("p h r t -> p (h r t)"), 256,
+                lambda shape, dtype, tag: stage_tile(shape, dtype, "h2" + tag[0], 4),
+            )
+
+        def suppress_mm(i, h):
+            h = int(h)
+            acc = acc_tile(("s3", int(i), h))
+            for q in range(2):
+                mx(acc[:], "k" + i, P * q, "su%d%d" % (q, h), 0, 512, q == 0, q == 1)
+
+        def gain(i, h, engine):
+            i, h = int(i), int(h)
+            if i not in t1:
+                t1[i] = stage_tile([P, 2, 512], F32, "t1", 4)
+            engines[engine].tensor_tensor(
+                out=t1[i][:, h, :].rearrange("p (b j i) -> p b j i", b=16, j=4),
+                in0=h2f[i][:, h, :].rearrange("p (j b i) -> p b j i", j=4, b=16),
+                in1=raw["af", i // 4][:, i % 4, 512 * h : 512 * h + 512].rearrange(
+                    "p (b j i) -> p b j i", b=16, j=4
+                ),
+                op=ALU.mult,
+            )
+
+        def gate(i, h):
+            i, h = int(i), int(h)
+            if i not in o_sb:
+                o_sb[i] = stage_tile([P, 2, 512], F32, "o", 4)
+            nc.vector.tensor_tensor(
+                out=o_sb[i][:, h, :],
+                in0=bank["s3", i, h][:],
+                in1=raw["ef", i // 4][:, i % 4, 512 * h : 512 * h + 512],
+                op=ALU.mult,
+            )
+
+        def finish(i, h, engine):
+            i, h = int(i), int(h)
+            engines[engine].tensor_tensor(
+                out=o_sb[i][:, h, :], in0=t1[i][:, h, :], in1=o_sb[i][:, h, :], op=ALU.subtract
+            )
+
+        def store(i, h):
+            i, h = int(i), int(h)
+            nc.sync.dma_start(
+                out=rows["out"][:, i // 4, i % 4, 512 * h : 512 * h + 512], in_=o_sb[i][:, h, :]
+            )
+
+        ops = {
+            "ld": load_rows, "lw": load_wt, "lu": load_su, "turn": turn, "evac": evac, "qr": quant_rows,
+            "weave": weave, "qw": quant_wt, "s1": spread_mm, "a1": spread_out,
+            "qh": h1_quant,
+            "s2": adapt_mm, "a2": adapt_out, "ht": h2_turn, "he": h2_evac, "hq": h2_quant,
+            "s3": suppress_mm, "t1": gain, "gt": gate, "fin": finish, "st": store,
+        }
+        for op in ORDER.split("\n"):
+            words = op.split(" ")
+            if words[0] in ops:
+                ops[words[0]](*words[1:])

from contextlib import ExitStack

import concourse.mybir as mybir
from concourse.masks import make_identity

F32 = mybir.dt.float32
BF16 = mybir.dt.bfloat16
U32 = mybir.dt.uint32
U8 = mybir.dt.uint8
FP8X4 = mybir.dt.float8_e4m3fn_x4
ALU = mybir.AluOpType

P = 128
C = 1024
FLOPS = 3 * 2 * C * C * C

ORDER = """
ld x 0
lw sp 0 0
ld x 1
lw sp 1 0
ld x 2
ld x 3
lw sp 0 1
lw sp 1 1
ld ad 0
turn x 0
ld ad 1
weave sp 0 0 3 s
weave sp 0 0 1 g
evac x 0 1 v
evac x 0 0 s
weave sp 0 0 2 g
ld ad 2
turn x 1
weave sp 0 0 0 s
qr x 0
weave sp 1 0 1 v
ld ad 3
weave sp 1 0 2 s
weave sp 1 0 3 v
evac x 1 0 s
weave sp 1 0 0 v
turn x 2
evac x 1 1 s
qw sp 0 0
qr x 1
turn x 3
evac x 2 1 s
qw sp 1 0
evac x 2 0 s
weave sp 0 1 3 v
s1 0 0 3
weave sp 0 1 0 s
qr x 2
s1 0 0 1
weave sp 0 1 2 s
weave sp 1 1 3 g
a1 0 0 3
s1 0 0 2
weave sp 0 1 1 s
a1 0 0 1
s1 0 0 0
evac x 3 1 s
a1 0 0 2
turn ad 0
lu 0 0
lu 0 1
lu 0 2
lu 0 3
lu 0 4
evac x 3 0 s
a1 0 0 0
lu 0 5
weave sp 1 1 2 s
qr x 3
turn ad 1
evac ad 0 0 s
qh 0 0
lu 0 6
s1 1 0 1
weave sp 1 1 0 s
qw sp 0 1
s1 1 0 3
evac ad 1 0 s
lu 0 7
a1 1 0 1
s1 1 0 0
evac ad 0 1 s
a1 1 0 3
s1 1 0 2
weave sp 1 1 1 s
a1 1 0 0
turn ad 2
evac ad 1 1 s
lu 1 0
lu 1 1
qr ad 0
lu 1 2
lu 1 3
lu 1 4
lu 1 5
lu 1 6
qw sp 1 1
turn ad 3
lu 1 7
weave su 0 0 3 s
weave su 0 0 1 v
weave su 0 0 0 s
weave su 0 1 3 g
a1 1 0 2
s1 0 1 1
weave su 0 1 2 s
s1 1 1 0
weave su 0 1 1 g
a1 0 1 1
ld af 0
evac ad 2 0 s
s1 0 1 0
ld af 1
qh 1 0
ld af 2
weave su 0 1 0 s
s1 1 1 3
ld af 3
ld ef 0
a1 1 1 0
s2 0 0
weave su 0 0 2 s
ld ef 1
ld ef 2
a1 1 1 3
ld ef 3
weave su 1 0 2 g
weave su 1 1 1 s
a1 0 1 0
s1 0 1 2
weave su 1 0 0 s
weave su 1 1 2 g
a2 0 0
s1 1 1 1
weave su 1 0 3 s
weave su 1 1 3 g
a1 0 1 2
s1 0 1 3
evac ad 2 1 s
weave su 1 0 1 g
a1 1 1 1
s1 1 1 2
evac ad 3 0 s
s2 1 0
a1 0 1 3
weave su 1 1 0 g
evac ad 3 1 s
a1 1 1 2
qw su 0 0
qh 1 1
qr ad 1
qh 0 1
s2 2 0
qr ad 2
s2 1 1
qw su 1 0
a2 2 0
s2 0 1
a2 1 0
qw su 0 1
s2 2 1
a2 0 1
t1 1 0 g
a2 1 1
ht 0
qr ad 3
ht 1
a2 2 1
t1 1 1 g
he 0 0 s
s2 3 0
he 1 1 s
he 1 0 v
he 0 1 s
qw su 1 1
s2 3 1
hq 1
a2 3 0
s3 1 1
hq 0
a2 3 1
t1 3 0 g
ht 2
gt 1 1
s3 0 1
he 2 0 s
t1 0 1 v
ht 3
he 2 1 s
t1 0 0 v
s3 0 0
hq 2
he 3 1 s
gt 0 1
fin 1 1 g
s3 2 0
he 3 0 s
gt 0 0
s3 1 0
fin 0 1 g
gt 2 0
s3 2 1
s2 4 0
gt 1 0
fin 0 0 v
s2 4 1
gt 2 1
fin 1 0 g
st 0 0
st 0 1
a2 4 0
s2 5 1
hq 3
st 1 0
st 1 1
t1 2 0 v
s3 3 1
t1 4 0 v
s2 5 0
a2 4 1
fin 2 0 g
gt 3 1
ht 4
t1 4 1 g
a2 5 0
st 2 0
s2 6 0
a2 5 1
he 4 0 s
t1 3 1 v
he 4 1 s
s3 3 0
t1 2 1 v
s2 6 1
hq 4
gt 3 0
fin 3 1 g
s3 4 1
a2 6 0
ht 5
fin 2 1 g
a2 6 1
gt 4 1
s3 4 0
he 5 0 s
fin 3 0 g
s2 7 1
st 2 1
he 5 1 s
gt 4 0
hq 5
ht 6
st 3 0
st 3 1
t1 5 0 v
s3 5 1
t1 5 1 v
he 6 0 s
s2 7 0
a2 7 1
fin 4 0 g
he 6 1 s
gt 5 1
s3 5 0
fin 4 1 g
a2 7 0
st 4 0
gt 5 0
ht 7
hq 6
st 4 1
fin 5 1 v
s3 6 0
he 7 1 s
t1 6 1 v
s3 6 1
he 7 0 s
t1 6 0 v
hq 7
gt 6 1
fin 5 0 g
s3 7 1
gt 6 0
s3 7 0
fin 6 1 g
gt 7 1
st 5 0
st 5 1
gt 7 0
fin 6 0 v
t1 7 0 v
st 6 0
st 6 1
t1 7 1 v
fin 7 0 v
fin 7 1 v
st 7 0
st 7 1
"""


def tile_cochlear_spread_adapt_suppress_t1_kernel(
    tc, x, spread, adapt, suppress, afferent, efferent, out
):
    nc = tc.nc
    rows = {}
    for key, ap in (("x", x), ("ad", adapt), ("af", afferent), ("ef", efferent), ("out", out)):
        rows[key] = ap.rearrange("(g p t) c -> p g t c", p=P, t=4)
    wts = {}
    for key, ap in (("sp", spread), ("su", suppress)):
        wts[key] = ap.rearrange("(q p j) c -> p q j c", p=P, j=4)

    with ExitStack() as ctx:
        keep = ctx.enter_context(tc.tile_pool(name="keep", bufs=1))
        stage = ctx.enter_context(tc.tile_pool(name="stage", bufs=2))
        psum = ctx.enter_context(tc.psum_pool(name="psum", bufs=4))
        ctx.enter_context(tc.manual_schedule())
        engines = {"v": nc.vector, "s": nc.scalar, "g": nc.gpsimd}

        def keep_tile(shape, dtype, tag):
            return keep.tile(shape, dtype, name=tag, tag=tag, align_bytes=64)

        def stage_tile(shape, dtype, tag, bufs):
            return stage.tile(shape, dtype, name=tag, tag=tag, bufs=bufs, align_bytes=64)

        ident = keep_tile([P, P], F32, "ident")
        make_identity(nc, ident[:])
        raw = {}
        bank = {}
        woven = {}
        codes = {}
        h2f = {}
        t1 = {}
        o_sb = {}

        def negate(engine, out, in_):
            if engine == "s":
                nc.scalar.mul(out, in_, -1.0)
            elif engine == "v":
                nc.vector.tensor_scalar_mul(out, in_, -1.0)
            else:
                nc.gpsimd.tensor_scalar(
                    out=out, in0=in_, scalar1=-1.0, scalar2=0.0, op0=ALU.mult, op1=ALU.add
                )

        def copy(engine, out, in_):
            if engine == "s":
                nc.scalar.copy(out=out, in_=in_)
            elif engine == "v":
                nc.vector.tensor_copy(out=out, in_=in_)
            else:
                nc.gpsimd.tensor_scalar(
                    out=out, in0=in_, scalar1=1.0, scalar2=0.0, op0=ALU.mult, op1=ALU.add
                )

        SLOT = {"x": "a", "ad": "c", "af": "c", "ef": "e"}

        def load_rows(key, c):
            c = int(c)
            g = c // 2
            h = 2 * (c % 2)
            if h == 0:
                raw[key, g] = keep_tile([P, 4, C], BF16, "%s%d" % (SLOT[key], g))
            nc.sync.dma_start(out=raw[key, g][:, h : h + 2, :], in_=rows[key][:, g, h : h + 2, :])

        def load_su(q, i):
            q, i = int(q), int(i)
            if i == 0:
                raw["su", q] = keep_tile([P, 4, C], BF16, "b%d" % q)
            nc.sync.dma_start(
                out=raw["su", q][i:P:8, :, :],
                in_=suppress[512 * q : 512 * q + 512, :].rearrange(
                    "(b j i) c -> i b j c", j=4, i=8
                )[i],
            )

        def load_wt(key, q, h):
            q, h = int(q), int(h)
            if h == 0:
                raw[key, q] = keep_tile([P, 4, C], BF16, "b%d" % q)
            nc.sync.dma_start(
                out=raw[key, q][:, :, 512 * h : 512 * h + 512],
                in_=wts[key][:, q, :, 512 * h : 512 * h + 512],
            )

        def turn(key, pr):
            b = psum.tile([P, 2, 2, 2, P], F32, name="tr", tag="tr", bufs=2)
            bank[key, pr] = b
            for k in range(2):
                i = 2 * int(pr) + k
                words = raw[key, i // 4][:, i % 4, :].bitcast(F32)
                for q in range(2):
                    for u in range(2):
                        nc.tensor.transpose(
                            b[:, k, q, u, :], words[:, 256 * q + u : 256 * (q + 1) : 2], ident[:]
                        )

        def evac(key, pr, k, engine):
            k = int(k)
            if (key, pr) not in woven:
                woven[key, pr] = stage_tile([P, 2, 1024], BF16, "rows_g", 3)
            copy(
                engine,
                woven[key, pr][:, k, :].bitcast(F32).rearrange("p (q r u) -> p q r u", q=2, u=2),
                bank[key, pr][:, k].rearrange("p q u r -> p q r u"),
            )

        def quantize(name, src_ap, words, pool_tile):
            c_t = pool_tile([P, words], U32, "c" + name)
            s_t = pool_tile([P, words], U8, "s" + name)
            nc.vector.quantize_mx(out=c_t[:].bitcast(FP8X4), scales=s_t[:], in_=src_ap)
            codes[name] = (c_t, s_t)

        def quant_rows(key, pr):
            quantize(
                key + pr, woven[key, pr][:].rearrange("p i e -> p (i e)"), 512, keep_tile
            )

        def weave(key, q, h, t, engine):
            q, h, t = int(q), int(h), int(t)
            if (key, q, h) not in woven:
                woven[key, q, h] = stage_tile([P, 2048], BF16, "w_g", 4)
            src = raw[key, q][:, :, 512 * h : 512 * h + 512]
            if key == "sp":
                o_v = woven[key, q, h][:].rearrange("p (t b i j) -> p t b i j", t=4, b=16, j=4)[:, t]
                i_v = src.rearrange("p j (b t i) -> p t b i j", b=16, t=4)[:, t]
            else:
                o_v = woven[key, q, h][:].rearrange("p (n j) -> p n j", j=4)
                o_v = o_v[:, P * t : P * (t + 1)]
                i_v = src.rearrange("p j n -> p n j")[:, P * t : P * (t + 1)]
            (negate if key == "sp" else copy)(engine, o_v, i_v)

        def quant_wt(key, q, h):
            quantize(key + q + h, woven[key, int(q), int(h)][:], 512, keep_tile)

        def mx(acc_ap, lhs, l0, rhs, r0, n, start, stop):
            nc.tensor.matmul_mx(
                out=acc_ap,
                lhsT=codes[lhs][0][:, l0 : l0 + P].bitcast(FP8X4),
                lhsT_scale=codes[lhs][1][:, l0 : l0 + P],
                rhs=codes[rhs][0][:, r0 : r0 + n].bitcast(FP8X4),
                rhs_scale=codes[rhs][1][:, r0 : r0 + n],
                start=start,
                stop=stop,
            )

        def acc_tile(key):
            bank[key] = psum.tile([P, 512], F32, name="acc", tag="acc", bufs=4)
            return bank[key]

        def x_perm(i, h):
            return raw["x", i // 4][:, i % 4, 512 * h : 512 * h + 512].rearrange(
                "p (b j i) -> p j b i", b=16, j=4
            )

        def spread_mm(g, h, j):
            g = int(g)
            acc = psum.tile([P, 4, P], F32, name="acc", tag="acc", bufs=4)
            bank["s1", g, h, j] = acc
            for t in range(4):
                i = 4 * g + t
                for q in range(2):
                    mx(
                        acc[:, t, :], "x%d" % (i // 2), 256 * (i % 2) + P * q,
                        "sp%d%s" % (q, h), P * int(j), P, q == 0, q == 1,
                    )

        def spread_out(g, h, j):
            g, hh, jj = int(g), int(h), int(j)
            if ("h1", g, h) not in woven:
                woven["h1", g, h] = stage_tile([P, 512, 4], BF16, "h1g", 3)
            nc.vector.tensor_tensor(
                out=woven["h1", g, h][:, P * jj : P * jj + P, :].rearrange(
                    "p (b i) t -> p b i t", i=8
                ),
                in0=raw["x", g][:, :, 512 * hh : 512 * hh + 512].rearrange(
                    "p t (b j i) -> p j b i t", b=16, j=4
                )[:, jj],
                in1=bank["s1", g, h, j][:].rearrange("p t (b i) -> p b i t", i=8),
                op=ALU.subtract,
            )

        def h1_quant(g, h):
            quantize(
                "h" + g + h, woven["h1", int(g), h][:].rearrange("p n t -> p (n t)"), 512,
                keep_tile,
            )

        def adapt_mm(i, h):
            i = int(i)
            acc = acc_tile(("s2", i, h))
            l0 = 256 * (i % 2)
            for q in range(2):
                mx(acc[:], "x%d" % (i // 2), l0 + P * q, "sp%d%s" % (q, h), 0, 512, q == 0, False)
            for q in range(2):
                mx(acc[:], "ad%d" % (i // 2), l0 + P * q, "h%d%s" % (q, h), 0, 512, False, q == 1)

        def adapt_out(i, h):
            i, hh = int(i), int(h)
            if i not in h2f:
                h2f[i] = stage_tile([P, 2, 512], F32, "h2f", 5)
            nc.vector.tensor_tensor(
                out=h2f[i][:, hh, :].rearrange("p (j b i) -> p j b i", j=4, b=16),
                in0=x_perm(i, hh),
                in1=bank["s2", i, h][:].rearrange("p (j b i) -> p j b i", j=4, b=16),
                op=ALU.subtract,
            )

        def h2_turn(i):
            b = psum.tile([P, 2, 4, P], F32, name="tr", tag="tr", bufs=2)
            bank["h2", i] = b
            for h in range(2):
                for t in range(4):
                    nc.tensor.transpose(
                        b[:, h, t, :], h2f[int(i)][:, h, P * t : P * t + P], ident[:]
                    )

        def h2_evac(i, h, engine):
            h = int(h)
            if ("h2", i) not in woven:
                woven["h2", i] = stage_tile([P, 2, P, 4], BF16, "h2g", 3)
            copy(engine, woven["h2", i][:, h], bank["h2", i][:, h].rearrange("p t r -> p r t"))

        def h2_quant(i):
            quantize(
                "k" + i, woven["h2", i][:].rearrange("p h r t -> p (h r t)"), 256,
                lambda shape, dtype, tag: stage_tile(shape, dtype, "h2" + tag[0], 4),
            )

        def suppress_mm(i, h):
            h = int(h)
            acc = acc_tile(("s3", int(i), h))
            for q in range(2):
                mx(acc[:], "k" + i, P * q, "su%d%d" % (q, h), 0, 512, q == 0, q == 1)

        def gain(i, h, engine):
            i, h = int(i), int(h)
            if i not in t1:
                t1[i] = stage_tile([P, 2, 512], F32, "t1", 4)
            engines[engine].tensor_tensor(
                out=t1[i][:, h, :].rearrange("p (b j i) -> p b j i", b=16, j=4),
                in0=h2f[i][:, h, :].rearrange("p (j b i) -> p b j i", j=4, b=16),
                in1=raw["af", i // 4][:, i % 4, 512 * h : 512 * h + 512].rearrange(
                    "p (b j i) -> p b j i", b=16, j=4
                ),
                op=ALU.mult,
            )

        def gate(i, h):
            i, h = int(i), int(h)
            if i not in o_sb:
                o_sb[i] = stage_tile([P, 2, 512], F32, "o", 4)
            nc.vector.tensor_tensor(
                out=o_sb[i][:, h, :],
                in0=bank["s3", i, h][:],
                in1=raw["ef", i // 4][:, i % 4, 512 * h : 512 * h + 512],
                op=ALU.mult,
            )

        def finish(i, h, engine):
            i, h = int(i), int(h)
            engines[engine].tensor_tensor(
                out=o_sb[i][:, h, :], in0=t1[i][:, h, :], in1=o_sb[i][:, h, :], op=ALU.subtract
            )

        def store(i, h):
            i, h = int(i), int(h)
            nc.sync.dma_start(
                out=rows["out"][:, i // 4, i % 4, 512 * h : 512 * h + 512], in_=o_sb[i][:, h, :]
            )

        ops = {
            "ld": load_rows, "lw": load_wt, "lu": load_su, "turn": turn, "evac": evac, "qr": quant_rows,
            "weave": weave, "qw": quant_wt, "s1": spread_mm, "a1": spread_out,
            "qh": h1_quant,
            "s2": adapt_mm, "a2": adapt_out, "ht": h2_turn, "he": h2_evac, "hq": h2_quant,
            "s3": suppress_mm, "t1": gain, "gt": gate, "fin": finish, "st": store,
        }
        for op in ORDER.split("\n"):
            words = op.split(" ")
            if words[0] in ops:
                ops[words[0]](*words[1:])
